import numpy as np
import ml_dtypes


def mxq(x, axis, fmt="e4m3"):
    dtype, down = {"e4m3": (ml_dtypes.float8_e4m3fn, 7), "e5m2": (ml_dtypes.float8_e5m2, 14)}[fmt]
    v = np.moveaxis(np.asarray(x, np.float32).astype(ml_dtypes.bfloat16).astype(np.float64), axis, -1)
    blocks = v.reshape(v.shape[:-1] + (-1, 32))
    amax = np.abs(blocks).max(-1, keepdims=True)
    byte = np.maximum(np.where(amax > 0, np.frexp(amax)[1] - 1 + 127, 0) - down, 1)
    scale = np.exp2(byte - 127.0)
    codes = (blocks / scale).astype(np.float32).astype(dtype).astype(np.float64)
    return np.moveaxis((codes * scale).reshape(v.shape), -1, axis)


WIDE = False


def mx_kscale(k):
    if not WIDE:
        return np.ones(k)
    levels = np.array([10, -10, 5, -5, 0])
    if k % 512:
        return np.exp2(np.random.permutation(np.resize(levels, k // 32))).repeat(32)
    a = np.empty((k // 512, 16))
    for p in range(k // 512):
        a[p, :8] = np.random.permutation(np.resize(levels, 8))
        for g in range(8):
            far = levels[np.abs(levels - a[p, g]) >= 10]
            a[p, g + 8] = far[np.random.randint(len(far))]
    return np.exp2(a.ravel()).repeat(32)


def f64(x):
    return np.asarray(x).astype(np.float64)


def striped(idx):
    return np.tile(np.asarray(idx).reshape(-1, 16).T, (8, 1)).astype(np.uint16)


def unstriped(offs):
    return offs[:16].T.reshape(-1).astype(np.int64)


E2M1 = np.array([0.0, 0.5, 1.0, 1.5, 2.0, 3.0, 4.0, 6.0, -0.0, -0.5, -1.0, -1.5, -2.0, -3.0, -4.0, -6.0])


def pack_weight(w, fmt):
    k, n = w.shape
    w = f64(np.asarray(w, np.float32).astype(ml_dtypes.bfloat16)).reshape(k // 32, 32, n)
    amax = np.abs(w).max(1)
    if fmt == "e4m3":
        byte = np.frexp(amax)[1] - 1 + 127 - 7
    else:
        mant, ex = np.frexp(amax / 6.0)
        byte = np.where(mant > 0.5, ex, ex - 1) + 127
    byte = np.clip(np.where(amax > 0, byte, 1), 1, 254)
    scaled = (w * np.exp2(127.0 - byte)[:, None, :]).reshape(k, n).astype(np.float32)
    by_word = np.ascontiguousarray(scaled.reshape(k // 512, 128, 4, n).transpose(0, 1, 3, 2))
    if fmt == "e4m3":
        words = by_word.astype(ml_dtypes.float8_e4m3fn).view(np.uint8)
    else:
        c = by_word.astype(ml_dtypes.float4_e2m1fn).view(np.uint8) & 0xF
        words = (c[..., 0::2] | (c[..., 1::2] << 4)).reshape(k // 512, 128, 2 * n)
    return np.ascontiguousarray(words), np.ascontiguousarray(byte.astype(np.uint8).reshape(k // 512, 16, n))


def unpack_weight(words, scales, fmt):
    g, _, n = scales.shape
    words = np.ascontiguousarray(words).reshape(g, 128, n, -1)
    if fmt == "e4m3":
        vals = words.view(ml_dtypes.float8_e4m3fn).astype(np.float64)
    else:
        nib = np.empty((g, 128, n, 4), np.uint8)
        nib[..., 0::2] = words & 0xF
        nib[..., 1::2] = words >> 4
        vals = E2M1[nib]
    vals = vals * np.repeat(np.exp2(scales.astype(np.float64) - 127.0), 8, axis=1)[..., None]
    return vals.transpose(0, 1, 3, 2).reshape(g * 512, n)


def softplus(v):
    return np.log(1.0 + np.exp(v))


def sigmoid(v):
    return 1.0 / (1.0 + np.exp(-v))


D, E, T, I, Q = 512, 512, 2048, 512, 128


def setup_inputs():
    n = np.random.standard_normal
    idx = np.random.permutation(T)[:I]
    fd = mx_kscale(D)
    fe = mx_kscale(E)
    fi = mx_kscale(I)
    ti = np.ones(T)
    ti[idx] = fi
    keysp = pack_weight(n((D, T)) / fd[:, None], "e2m1")
    valsp = pack_weight(n((E, T)) / fe[:, None], "e2m1")
    return {
        "query": (n((D, Q)) * 1.0 / np.sqrt(D) * fd[:, None]).astype(np.float32),
        "keys_words": keysp[0],
        "keys_scales": keysp[1],
        "th": (np.random.uniform(-0.5, 0.5, (Q, 1))).astype(np.float32),
        "reserve": (np.random.uniform(20.0, 100.0, (Q, 1))).astype(np.float32),
        "gout": (n((E, Q)) * 1 / np.sqrt(E) * fe[:, None]).astype(np.float32),
        "vals_words": valsp[0],
        "vals_scales": valsp[1],
        "size": (np.random.uniform(0.5, 2.0, (1, I))).astype(np.float32),
        "fs": (np.random.uniform(128.0, 512.0, (1, I)) * fi).astype(np.float32),
        "keyrows": (n((D, T)) / ti).astype(np.float32),
        "res": (n((Q, D)) * 4.0).astype(np.float32),
        "offs": striped(idx),
    }


def reference(query, keys_words, keys_scales, th, reserve, gout, vals_words, vals_scales, size, fs, keyrows, res, offs):
    idx = unstriped(offs)
    keysu = unpack_weight(keys_words, keys_scales, "e2m1")
    valsu = unpack_weight(vals_words, vals_scales, "e2m1")
    queryq = mxq(f64(query), 0, "e4m3")
    keysidxg = keysu[:, idx]
    a = queryq.T @ keysidxg
    p = softplus(a - f64(th))
    z = np.sum(p, axis=1, keepdims=True) + f64(reserve)
    goutq = mxq(f64(gout), 0, "e4m3")
    valsidxg = valsu[:, idx]
    c0 = goutq.T @ valsidxg
    dz = np.sum(c0 * p * f64(size) / np.square(z) * (-1.0), axis=1, keepdims=True)
    dp = c0 / z * f64(size) + dz
    da = dp * sigmoid(a - f64(th))
    gs = da * f64(fs)
    gt1 = gs.T
    kt = f64(keyrows)[:, idx].T
    gt1q = mxq(gt1, 0, "e4m3")
    ktq = mxq(kt, 0, "e4m3")
    gq = gt1q.T @ ktq
    y = gq + f64(res)
    return y

@@ -1,0 +1,226 @@
+from contextlib import ExitStack
+
+import concourse.mybir as mybir
+from concourse.masks import make_identity
+
+D, E, T, I, Q = 512, 512, 2048, 512, 128
+FLOPS = 3 * 2 * 512 * 512 * 128
+
+F32 = mybir.dt.float32
+BF16 = mybir.dt.bfloat16
+I32 = mybir.dt.int32
+U32 = mybir.dt.uint32
+U16 = mybir.dt.uint16
+U8 = mybir.dt.uint8
+FP8X4 = mybir.dt.float8_e4m3fn_x4
+FP4X4 = mybir.dt.float4_e2m1fn_x4
+ACT = mybir.ActivationFunctionType
+ALU = mybir.AluOpType
+
+P = 128
+PACK = 4
+BLOCKS = D // P
+REUSE = {"c_words": "q_raw", "cs": "key_pool0", "cast": "off_half", "kt0_grouped": "z_part", "picked2": "wz",
+         "gs_codes": "key_pool2", "late_codes": "key_pool3"}
+
+
+def tile_attend_bsoftthreshold_q_kernel(tc, query, keys_words, keys_scales, th, reserve, gout,
+                                         vals_words, vals_scales, size, fs, keyrows, res, offs, out):
+    nc = tc.nc
+    with ExitStack() as ctx:
+        sb = ctx.enter_context(tc.tile_pool(name="sb", bufs=1))
+        ps = ctx.enter_context(tc.psum_pool(name="ps", bufs=1))
+
+        def sbuf(name, shape, dtype):
+            return sb.tile(shape, dtype, name=name, tag=REUSE.get(name, name), align_bytes=64)
+
+        offsets = sbuf("offsets", [P, I // 16], U16)
+        nc.sync.dma_start(offsets[:], offs)
+
+        def load_words(name, words):
+            pool_words = sbuf(name, [P, T], U16)
+            nc.sync.dma_start(out=pool_words[:].bitcast(I32), in_=words[0].bitcast(I32))
+            return pool_words
+
+        def load_scales(name, scales):
+            pool_scales = sbuf(name, [P, T], U8)
+            nc.vector.memset(pool_scales[:].bitcast(I32), 0)
+            for quad in range(4):
+                nc.sync.dma_start(out=pool_scales[32 * quad : 32 * quad + 4, :].bitcast(I32),
+                                  in_=scales[0, 4 * quad : 4 * quad + 4, :].bitcast(I32))
+            return pool_scales
+
+        def load_scales_repeated(name, scales):
+            pool_scales = sbuf(name, [P, T], U8)
+            for quad in range(4):
+                nc.sync.dma_start(out=pool_scales[32 * quad : 32 * quad + 32, :].bitcast(I32),
+                                  in_=scales[:, 4 * quad : 4 * quad + 4, :].bitcast(I32).to_broadcast([8, 4, T // 4]))
+            return pool_scales
+
+        def load_rows(name, rows):
+            raw = sbuf(name, [P, PACK, Q], F32)
+            nc.sync.dma_start(out=raw[:], in_=rows.rearrange("(p j) w -> p j w", j=PACK))
+            return raw
+
+        def load_small(name, src, width, queue):
+            small = sbuf(name, [P, width], F32)
+            queue.dma_start(out=small[:], in_=src)
+            return small
+
+        small = {}
+        th_col = load_small("th_col", th, 1, nc.gpsimd)
+        ident = sbuf("ident", [P, P], F32)
+        make_identity(nc, ident[:])
+        small["reserve"] = load_small("reserve_col", reserve, 1, nc.gpsimd)
+
+        warm_in = sbuf("warm_in", [P, 1], F32)
+        nc.vector.memset(warm_in[:], 0.0)
+        warm = sbuf("warm", [P, 1], F32)
+        nc.scalar.activation(out=warm[:], in_=warm_in[:], func=ACT.Sigmoid)
+
+        keys_w = load_words("keys_w", keys_words)
+        small["size"] = load_small("size_col", size.rearrange("o (p c) -> p (o c)", c=PACK), PACK, nc.sync)
+        keys_s = load_scales_repeated("keys_s", keys_scales)
+        q_raw = load_rows("q_raw", query)
+        vals_w = load_words("vals_w", vals_words)
+        vals_s = load_scales("vals_s", vals_scales)
+        g_raw = load_rows("g_raw", gout)
+        key_pool = []
+        for b in range(BLOCKS):
+            rows = sbuf("key_pool%d" % b, [P, T], F32)
+            nc.sync.dma_start(out=rows[:], in_=keyrows[b * P : (b + 1) * P, :])
+            key_pool.append(rows)
+            if b == 0:
+                small["fs"] = load_small("fs_col", fs.rearrange("o (p c) -> p (o c)", c=PACK), PACK, nc.sync)
+        res_sb = sbuf("res_sb", [P, D], F32)
+        nc.sync.dma_start(out=res_sb[:], in_=res)
+
+        def quantize(name, grouped, width):
+            codes = sbuf(name + "_codes", [P, width], U32)
+            scales = sbuf(name + "_scales", [P, width], U8)
+            nc.vector.quantize_mx(out=codes[:].bitcast(FP8X4), scales=scales[:], in_=grouped)
+            return codes, scales
+
+        def score(name, raw, pool_words, pool_scales):
+            words = sbuf(name + "_words", [P, I], U16)
+            nc.vector.tensor_copy(out=words[:], in_=pool_words[:].indirect(offsets[:]))
+            scale_bytes = sbuf(name + "_bytes", [P, I], U8)
+            nc.vector.tensor_copy(out=scale_bytes[:], in_=pool_scales[:].indirect(offsets[:]))
+            grouped = sbuf(name + "_grouped", [P, Q, PACK], BF16)
+            nc.scalar.copy(out=grouped[:], in_=raw[:].rearrange("p j w -> p w j"))
+            codes, scales = quantize(name, grouped[:].rearrange("p w j -> p (w j)"), Q)
+            acc = ps.tile([P, I], F32, name=name + "_acc", tag=name + "_bank")
+            nc.tensor.matmul_mx(out=acc[:], lhsT=codes[:].bitcast(FP8X4), lhsT_scale=scales[:],
+                                rhs=words[:].bitcast(FP4X4), rhs_scale=scale_bytes[:], start=True, stop=True)
+            return acc
+
+        def spread(name, col, bank):
+            rows = ps.tile([P, PACK, P], F32, name=name, tag=bank)
+            for c in range(PACK):
+                nc.tensor.transpose(rows[:, c, :], col[:, c : c + 1].to_broadcast([P, P]), ident[:])
+            return rows[:].rearrange("p c s -> p s c")
+
+        def by_four(tile):
+            return tile[:].rearrange("p (s c) -> p s c", c=PACK)
+
+        neg_th = sbuf("neg_th", [P, 1], F32)
+        nc.scalar.activation(out=neg_th[:], in_=th_col[:], func=ACT.Copy, scale=-1.0)
+
+        a = score("a", q_raw, keys_w, keys_s)
+        sig = sbuf("sig", [P, I], F32)
+        nc.scalar.activation(out=sig[:], in_=a[:], func=ACT.Sigmoid, bias=neg_th[:])
+        hinge = sbuf("hinge", [P, I], F32)
+        hinge_sum = sbuf("hinge_sum", [P, 1], F32)
+        nc.scalar.activation(out=hinge[:], in_=a[:], func=ACT.Relu, bias=neg_th[:], accum_out=hinge_sum[:])
+        off_half = sbuf("off_half", [P, I], F32)
+        nc.scalar.activation(out=off_half[:], in_=sig[:], func=ACT.Abs, bias=-0.5)
+
+        c0 = score("c", g_raw, vals_w, vals_s)
+        size_ps = spread("size_ps", small["size"], "size_ps_bank")
+        size_rows = sbuf("size_rows", [P, I], F32)
+        nc.scalar.copy(out=by_four(size_rows), in_=size_ps)
+
+        z_part = sbuf("z_part", [P, 1], F32)
+        nc.scalar.activation(out=z_part[:], in_=hinge_sum[:], func=ACT.Identity, bias=small["reserve"][:])
+        log_term = sbuf("log_term", [P, I], F32)
+        log_sum = sbuf("log_sum", [P, 1], F32)
+        nc.scalar.activation(out=log_term[:], in_=off_half[:], func=ACT.Ln, bias=0.5, accum_out=log_sum[:])
+        z = sbuf("z", [P, 1], F32)
+        nc.scalar.activation(out=z[:], in_=log_sum[:], func=ACT.Identity, scale=-1.0, bias=z_part[:])
+
+        first_picked = sbuf("picked0", [P, I], BF16)
+        nc.vector.tensor_copy(out=first_picked[:], in_=key_pool[0][:].indirect(offsets[:]))
+        cs = sbuf("cs", [P, I], F32)
+        nc.vector.tensor_tensor(out=cs[:], in0=c0[:], in1=size_rows[:], op=ALU.mult)
+        fs_ps = spread("fs_ps", small["fs"], "c_bank")
+        scrap = sbuf("scrap", [P, I], F32)
+        s_hinge = sbuf("s_hinge", [P, 1], F32)
+        nc.vector.scalar_tensor_tensor(out=scrap[:], in0=hinge[:], scalar=1.0, in1=cs[:], op0=ALU.mult, op1=ALU.mult,
+                                       accum_out=s_hinge[:])
+        rz = sbuf("rz", [P, 1], F32)
+        nc.vector.reciprocal(out=rz[:], in_=z[:])
+        scrap2 = sbuf("scrap2", [P, I], F32)
+        s_log = sbuf("s_log", [P, 1], F32)
+        nc.vector.scalar_tensor_tensor(out=scrap2[:], in0=log_term[:], scalar=1.0, in1=cs[:], op0=ALU.mult, op1=ALU.mult,
+                                       accum_out=s_log[:])
+        wz = sbuf("wz", [P, I], F32)
+        nc.vector.scalar_tensor_tensor(out=by_four(wz), in0=by_four(sig), scalar=rz[:], in1=fs_ps, op0=ALU.mult, op1=ALU.mult)
+        mean = sbuf("mean", [P, 1], F32)
+        nc.vector.tensor_scalar(out=mean[:], in0=s_hinge[:], scalar1=s_log[:], scalar2=rz[:], op0=ALU.subtract, op1=ALU.mult)
+        gs = sbuf("gs", [P, I], BF16)
+        nc.vector.scalar_tensor_tensor(out=gs[:], in0=cs[:], scalar=mean[:], in1=wz[:], op0=ALU.subtract, op1=ALU.mult)
+
+        def turn(name, rows, bank, grouped):
+            words = rows[:].bitcast(F32)
+            turned = ps.tile([P, 2, P], F32, name=name + "_turned", tag=bank)
+            for u in range(2):
+                nc.tensor.transpose(turned[:, u, :], words[:, u : I // 2 : 2], ident[:])
+            nc.scalar.copy(out=grouped.bitcast(F32), in_=turned[:].rearrange("p u r -> p r u"))
+
+        def flat(grouped):
+            return grouped[:].rearrange("p r j -> p (r j)")
+
+        kt0_grouped = sbuf("kt0_grouped", [P, P, PACK], BF16)
+        turn("kt0", first_picked, "kt_bank0", kt0_grouped[:])
+        kt0_codes, kt0_scales = quantize("kt0", flat(kt0_grouped), P)
+
+        kt12_grouped = sbuf("kt12_grouped", [P, 2 * P, PACK], BF16)
+        cast = sbuf("cast", [P, T], BF16)
+        for piece in range(4):
+            part = slice(piece * 512, (piece + 1) * 512)
+            nc.scalar.activation(out=cast[:, part], in_=key_pool[1][:, part], func=ACT.Copy)
+        picked1 = sbuf("picked1", [P, I], BF16)
+        nc.scalar.activation(out=picked1[:], in_=cast[:].indirect(offsets[:]), func=ACT.Copy)
+
+        picked2 = sbuf("picked2", [P, I], BF16)
+        nc.vector.tensor_copy(out=picked2[:], in_=key_pool[2][:].indirect(offsets[:]))
+
+        gs_grouped = sbuf("gs_grouped", [P, Q, PACK], BF16)
+        turn("gs", gs, "size_ps_bank", gs_grouped[:])
+        gs_codes, gs_scales = quantize("gs", flat(gs_grouped), Q)
+
+        picked3 = sbuf("picked3", [P, I], BF16)
+        nc.vector.tensor_copy(out=picked3[:], in_=key_pool[3][:].indirect(offsets[:]))
+
+        turn("kt1", picked1, "kt_bank1", kt12_grouped[:, 0:P, :])
+        turn("kt2", picked2, "kt_bank0", kt12_grouped[:, P : 2 * P, :])
+        kt3_grouped = sbuf("kt3_grouped", [P, P, PACK], BF16)
+        turn("kt3", picked3, "kt_bank1", kt3_grouped[:])
+
+        late_codes = sbuf("late_codes", [P, 3 * P], U32)
+        late_scales = sbuf("late_scales", [P, 3 * P], U8)
+        nc.vector.quantize_mx(out=late_codes[:, 0 : 2 * P].bitcast(FP8X4), scales=late_scales[:, 0 : 2 * P], in_=flat(kt12_grouped))
+        nc.vector.quantize_mx(out=late_codes[:, 2 * P :].bitcast(FP8X4), scales=late_scales[:, 2 * P :], in_=flat(kt3_grouped))
+
+        for name, cols, codes, scales, bank in (
+            ("o0", slice(0, P), kt0_codes[:], kt0_scales[:], "a_bank"),
+            ("o1", slice(P, 3 * P), late_codes[:, 0 : 2 * P], late_scales[:, 0 : 2 * P], "c_bank"),
+            ("o2", slice(3 * P, D), late_codes[:, 2 * P :], late_scales[:, 2 * P :], "last_bank"),
+        ):
+            width = cols.stop - cols.start
+            acc = ps.tile([P, width], F32, name=name + "_acc", tag=bank)
+            nc.tensor.matmul_mx(out=acc[:], lhsT=gs_codes[:].bitcast(FP8X4), lhsT_scale=gs_scales[:],
+                                rhs=codes.bitcast(FP8X4), rhs_scale=scales, start=True, stop=True)
+            result = sbuf(name, [P, width], F32)
+            nc.vector.tensor_tensor(out=result[:], in0=acc[:], in1=res_sb[:, cols], op=ALU.add)
+            nc.sync.dma_start(out=out[:, cols], in_=result[:])

@@ -20,8 +20,8 @@ ALU = mybir.AluOpType
 P = 128
 PACK = 4
 BLOCKS = D // P
-REUSE = {"c_words": "q_raw", "cs": "key_pool0", "cast": "off_half", "kt0_grouped": "z_part", "picked2": "wz",
-         "gs_codes": "key_pool2", "late_codes": "key_pool3"}
+REUSE = {"c_words": "g_raw", "cs": "key_pool0", "cast": "off_half", "kt0_grouped": "z_part", "picked2": "wz",
+         "late_codes": "key_pool3", "gs_grouped": "key_pool1", "log_term": "size_col"}
 
 
 def tile_attend_bsoftthreshold_q_kernel(tc, query, keys_words, keys_scales, th, reserve, gout,
@@ -68,10 +68,8 @@ def tile_attend_bsoftthreshold_q_kernel(tc, query, keys_words, keys_scales, th, 
             return small
 
         small = {}
-        th_col = load_small("th_col", th, 1, nc.gpsimd)
         ident = sbuf("ident", [P, P], F32)
         make_identity(nc, ident[:])
-        small["reserve"] = load_small("reserve_col", reserve, 1, nc.gpsimd)
 
         warm_in = sbuf("warm_in", [P, 1], F32)
         nc.vector.memset(warm_in[:], 0.0)
@@ -79,12 +77,13 @@ def tile_attend_bsoftthreshold_q_kernel(tc, query, keys_words, keys_scales, th, 
         nc.scalar.activation(out=warm[:], in_=warm_in[:], func=ACT.Sigmoid)
 
         keys_w = load_words("keys_w", keys_words)
-        small["size"] = load_small("size_col", size.rearrange("o (p c) -> p (o c)", c=PACK), PACK, nc.sync)
         keys_s = load_scales_repeated("keys_s", keys_scales)
         q_raw = load_rows("q_raw", query)
-        vals_w = load_words("vals_w", vals_words)
-        vals_s = load_scales("vals_s", vals_scales)
         g_raw = load_rows("g_raw", gout)
+        vals_w = load_words("vals_w", vals_words)
+        th_col = load_small("th_col", th, 1, nc.sync)
+        small["size"] = load_small("size_col", size.rearrange("o (p c) -> p (o c)", c=PACK), PACK, nc.sync)
+        vals_s = load_scales("vals_s", vals_scales)
         key_pool = []
         for b in range(BLOCKS):
             rows = sbuf("key_pool%d" % b, [P, T], F32)
@@ -92,6 +91,7 @@ def tile_attend_bsoftthreshold_q_kernel(tc, query, keys_words, keys_scales, th, 
             key_pool.append(rows)
             if b == 0:
                 small["fs"] = load_small("fs_col", fs.rearrange("o (p c) -> p (o c)", c=PACK), PACK, nc.sync)
+                small["reserve"] = load_small("reserve_col", reserve, 1, nc.sync)
         res_sb = sbuf("res_sb", [P, D], F32)
         nc.sync.dma_start(out=res_sb[:], in_=res)
 
@@ -101,16 +101,16 @@ def tile_attend_bsoftthreshold_q_kernel(tc, query, keys_words, keys_scales, th, 
             nc.vector.quantize_mx(out=codes[:].bitcast(FP8X4), scales=scales[:], in_=grouped)
             return codes, scales
 
-        def score(name, raw, pool_words, pool_scales):
+        def gather_packed(name, pool_words, pool_scales):
             words = sbuf(name + "_words", [P, I], U16)
             nc.vector.tensor_copy(out=words[:], in_=pool_words[:].indirect(offsets[:]))
             scale_bytes = sbuf(name + "_bytes", [P, I], U8)
             nc.vector.tensor_copy(out=scale_bytes[:], in_=pool_scales[:].indirect(offsets[:]))
-            grouped = sbuf(name + "_grouped", [P, Q, PACK], BF16)
-            nc.scalar.copy(out=grouped[:], in_=raw[:].rearrange("p j w -> p w j"))
-            codes, scales = quantize(name, grouped[:].rearrange("p w j -> p (w j)"), Q)
+            return words, scale_bytes
+
+        def score(name, codes, scales, words, scale_bytes):
             acc = ps.tile([P, I], F32, name=name + "_acc", tag=name + "_bank")
-            nc.tensor.matmul_mx(out=acc[:], lhsT=codes[:].bitcast(FP8X4), lhsT_scale=scales[:],
+            nc.tensor.matmul_mx(out=acc[:], lhsT=codes.bitcast(FP8X4), lhsT_scale=scales,
                                 rhs=words[:].bitcast(FP4X4), rhs_scale=scale_bytes[:], start=True, stop=True)
             return acc
 
@@ -126,7 +126,12 @@ def tile_attend_bsoftthreshold_q_kernel(tc, query, keys_words, keys_scales, th, 
         neg_th = sbuf("neg_th", [P, 1], F32)
         nc.scalar.activation(out=neg_th[:], in_=th_col[:], func=ACT.Copy, scale=-1.0)
 
-        a = score("a", q_raw, keys_w, keys_s)
+        a_words, a_bytes = gather_packed("a", keys_w, keys_s)
+        qg_grouped = sbuf("qg_grouped", [P, 2 * Q, PACK], BF16)
+        nc.scalar.copy(out=qg_grouped[:, 0:Q, :], in_=q_raw[:].rearrange("p j w -> p w j"))
+        nc.scalar.copy(out=qg_grouped[:, Q : 2 * Q, :], in_=g_raw[:].rearrange("p j w -> p w j"))
+        qg_codes, qg_scales = quantize("qg", qg_grouped[:].rearrange("p w j -> p (w j)"), 2 * Q)
+        a = score("a", qg_codes[:, 0:Q], qg_scales[:, 0:Q], a_words, a_bytes)
         sig = sbuf("sig", [P, I], F32)
         nc.scalar.activation(out=sig[:], in_=a[:], func=ACT.Sigmoid, bias=neg_th[:])
         hinge = sbuf("hinge", [P, I], F32)
@@ -135,7 +140,8 @@ def tile_attend_bsoftthreshold_q_kernel(tc, query, keys_words, keys_scales, th, 
         off_half = sbuf("off_half", [P, I], F32)
         nc.scalar.activation(out=off_half[:], in_=sig[:], func=ACT.Abs, bias=-0.5)
 
-        c0 = score("c", g_raw, vals_w, vals_s)
+        c_words, c_bytes = gather_packed("c", vals_w, vals_s)
+        c0 = score("c", qg_codes[:, Q : 2 * Q], qg_scales[:, Q : 2 * Q], c_words, c_bytes)
         size_ps = spread("size_ps", small["size"], "size_ps_bank")
         size_rows = sbuf("size_rows", [P, I], F32)
         nc.scalar.copy(out=by_four(size_rows), in_=size_ps)
@@ -197,7 +203,6 @@ def tile_attend_bsoftthreshold_q_kernel(tc, query, keys_words, keys_scales, th, 
 
         gs_grouped = sbuf("gs_grouped", [P, Q, PACK], BF16)
         turn("gs", gs, "size_ps_bank", gs_grouped[:])
-        gs_codes, gs_scales = quantize("gs", flat(gs_grouped), Q)
 
         picked3 = sbuf("picked3", [P, I], BF16)
         nc.vector.tensor_copy(out=picked3[:], in_=key_pool[3][:].indirect(offsets[:]))
@@ -207,19 +212,21 @@ def tile_attend_bsoftthreshold_q_kernel(tc, query, keys_words, keys_scales, th, 
         kt3_grouped = sbuf("kt3_grouped", [P, P, PACK], BF16)
         turn("kt3", picked3, "kt_bank1", kt3_grouped[:])
 
-        late_codes = sbuf("late_codes", [P, 3 * P], U32)
-        late_scales = sbuf("late_scales", [P, 3 * P], U8)
+        late_codes = sbuf("late_codes", [P, 4 * P], U32)
+        late_scales = sbuf("late_scales", [P, 4 * P], U8)
+        gs_codes, gs_scales = late_codes[:, 3 * P :], late_scales[:, 3 * P :]
+        nc.vector.quantize_mx(out=gs_codes.bitcast(FP8X4), scales=gs_scales, in_=flat(gs_grouped))
         nc.vector.quantize_mx(out=late_codes[:, 0 : 2 * P].bitcast(FP8X4), scales=late_scales[:, 0 : 2 * P], in_=flat(kt12_grouped))
-        nc.vector.quantize_mx(out=late_codes[:, 2 * P :].bitcast(FP8X4), scales=late_scales[:, 2 * P :], in_=flat(kt3_grouped))
+        nc.vector.quantize_mx(out=late_codes[:, 2 * P : 3 * P].bitcast(FP8X4), scales=late_scales[:, 2 * P : 3 * P], in_=flat(kt3_grouped))
 
         for name, cols, codes, scales, bank in (
             ("o0", slice(0, P), kt0_codes[:], kt0_scales[:], "a_bank"),
             ("o1", slice(P, 3 * P), late_codes[:, 0 : 2 * P], late_scales[:, 0 : 2 * P], "c_bank"),
-            ("o2", slice(3 * P, D), late_codes[:, 2 * P :], late_scales[:, 2 * P :], "last_bank"),
+            ("o2", slice(3 * P, D), late_codes[:, 2 * P : 3 * P], late_scales[:, 2 * P : 3 * P], "last_bank"),
         ):
             width = cols.stop - cols.start
             acc = ps.tile([P, width], F32, name=name + "_acc", tag=bank)
-            nc.tensor.matmul_mx(out=acc[:], lhsT=gs_codes[:].bitcast(FP8X4), lhsT_scale=gs_scales[:],
+            nc.tensor.matmul_mx(out=acc[:], lhsT=gs_codes.bitcast(FP8X4), lhsT_scale=gs_scales,
                                 rhs=codes.bitcast(FP8X4), rhs_scale=scales, start=True, stop=True)
             result = sbuf(name, [P, width], F32)
             nc.vector.tensor_tensor(out=result[:], in0=acc[:], in1=res_sb[:, cols], op=ALU.add)

@@ -3,8 +3,8 @@ from contextlib import ExitStack
 import concourse.mybir as mybir
 from concourse.masks import make_identity
 
-D, E, T, I, Q = 512, 512, 2048, 512, 128
-FLOPS = 3 * 2 * 512 * 512 * 128
+D, T, I, Q = 512, 2048, 512, 128
+FLOPS = 3 * 2 * Q * D * I
 
 F32 = mybir.dt.float32
 BF16 = mybir.dt.bfloat16
@@ -19,9 +19,23 @@ ALU = mybir.AluOpType
 
 P = 128
 PACK = 4
-BLOCKS = D // P
-REUSE = {"c_words": "g_raw", "cs": "key_pool0", "cast": "off_half", "kt0_grouped": "z_part", "picked2": "wz",
-         "late_codes": "key_pool3", "gs_grouped": "key_pool1", "log_term": "size_col"}
+QUADRANTS = 4
+CAST_PIECE = 512
+
+TAKES_OVER = {
+    "vals_words_picked": "query_raw",
+    "gout_grouped": "size_col",
+    "log_term": "gout_raw",
+    "cs": "key_rows0",
+    "cast_rows": "off_half",
+    "log_product": "log_sum",
+    "kt0_grouped": "z_part",
+    "kt0_codes": "log_sum",
+    "picked2": "log_dot",
+    "gs_grouped": "key_rows1",
+    "late_codes": "key_rows3",
+    "out_early": "kt3_grouped",
+}
 
 
 def tile_attend_bsoftthreshold_q_kernel(tc, query, keys_words, keys_scales, th, reserve, gout,
@@ -32,106 +46,108 @@ def tile_attend_bsoftthreshold_q_kernel(tc, query, keys_words, keys_scales, th, 
         ps = ctx.enter_context(tc.psum_pool(name="ps", bufs=1))
 
         def sbuf(name, shape, dtype):
-            return sb.tile(shape, dtype, name=name, tag=REUSE.get(name, name), align_bytes=64)
+            return sb.tile(shape, dtype, name=name, tag=TAKES_OVER.get(name, name), align_bytes=64)
 
-        offsets = sbuf("offsets", [P, I // 16], U16)
-        nc.sync.dma_start(offsets[:], offs)
+        def load(name, shape, dtype, src):
+            tile = sbuf(name, shape, dtype)
+            nc.sync.dma_start(out=tile[:], in_=src)
+            return tile
 
         def load_words(name, words):
-            pool_words = sbuf(name, [P, T], U16)
-            nc.sync.dma_start(out=pool_words[:].bitcast(I32), in_=words[0].bitcast(I32))
-            return pool_words
+            tile = sbuf(name, [P, T], U16)
+            nc.sync.dma_start(out=tile[:].bitcast(I32), in_=words[0].bitcast(I32))
+            return tile
 
-        def load_scales(name, scales):
-            pool_scales = sbuf(name, [P, T], U8)
-            nc.vector.memset(pool_scales[:].bitcast(I32), 0)
-            for quad in range(4):
-                nc.sync.dma_start(out=pool_scales[32 * quad : 32 * quad + 4, :].bitcast(I32),
+        def load_scales(name, scales, second_half_engine):
+            tile = sbuf(name, [P, T], U8)
+            nc.vector.memset(tile[:, : T // 2].bitcast(I32), 0)
+            second_half_engine.memset(tile[:, T // 2 :].bitcast(I32), 0)
+            for quad in range(QUADRANTS):
+                nc.sync.dma_start(out=tile[32 * quad : 32 * quad + 4, :].bitcast(I32),
                                   in_=scales[0, 4 * quad : 4 * quad + 4, :].bitcast(I32))
-            return pool_scales
+            return tile
 
-        def load_scales_repeated(name, scales):
-            pool_scales = sbuf(name, [P, T], U8)
-            for quad in range(4):
-                nc.sync.dma_start(out=pool_scales[32 * quad : 32 * quad + 32, :].bitcast(I32),
-                                  in_=scales[:, 4 * quad : 4 * quad + 4, :].bitcast(I32).to_broadcast([8, 4, T // 4]))
-            return pool_scales
+        def four_rows_a_partition(rows):
+            return rows.rearrange("(p t) w -> p t w", t=PACK)
 
-        def load_rows(name, rows):
-            raw = sbuf(name, [P, PACK, Q], F32)
-            nc.sync.dma_start(out=raw[:], in_=rows.rearrange("(p j) w -> p j w", j=PACK))
-            return raw
+        def four_slots_a_partition(row):
+            return row.rearrange("o (p t) -> p (o t)", t=PACK)
 
-        def load_small(name, src, width, queue):
-            small = sbuf(name, [P, width], F32)
-            queue.dma_start(out=small[:], in_=src)
-            return small
+        offsets = load("offsets", [P, I // 16], U16, offs)
+        keys_w = load_words("keys_w", keys_words)
+        keys_s = load_scales("keys_s", keys_scales, nc.gpsimd)
 
-        small = {}
+        warm_in = sbuf("warm_in", [P, 1], F32)
+        nc.gpsimd.memset(warm_in[:], 0.0)
+        warm_out = sbuf("warm_out", [P, 1], F32)
+        nc.scalar.activation(out=warm_out[:], in_=warm_in[:], func=ACT.Sigmoid)
         ident = sbuf("ident", [P, P], F32)
         make_identity(nc, ident[:])
 
-        warm_in = sbuf("warm_in", [P, 1], F32)
-        nc.vector.memset(warm_in[:], 0.0)
-        warm = sbuf("warm", [P, 1], F32)
-        nc.scalar.activation(out=warm[:], in_=warm_in[:], func=ACT.Sigmoid)
-
-        keys_w = load_words("keys_w", keys_words)
-        keys_s = load_scales_repeated("keys_s", keys_scales)
-        q_raw = load_rows("q_raw", query)
-        g_raw = load_rows("g_raw", gout)
+        query_raw = load("query_raw", [P, PACK, Q], F32, four_rows_a_partition(query))
+        size_col = load("size_col", [P, PACK], F32, four_slots_a_partition(size))
         vals_w = load_words("vals_w", vals_words)
-        th_col = load_small("th_col", th, 1, nc.sync)
-        small["size"] = load_small("size_col", size.rearrange("o (p c) -> p (o c)", c=PACK), PACK, nc.sync)
-        vals_s = load_scales("vals_s", vals_scales)
-        key_pool = []
-        for b in range(BLOCKS):
-            rows = sbuf("key_pool%d" % b, [P, T], F32)
-            nc.sync.dma_start(out=rows[:], in_=keyrows[b * P : (b + 1) * P, :])
-            key_pool.append(rows)
-            if b == 0:
-                small["fs"] = load_small("fs_col", fs.rearrange("o (p c) -> p (o c)", c=PACK), PACK, nc.sync)
-                small["reserve"] = load_small("reserve_col", reserve, 1, nc.sync)
-        res_sb = sbuf("res_sb", [P, D], F32)
-        nc.sync.dma_start(out=res_sb[:], in_=res)
+        gout_raw = load("gout_raw", [P, PACK, Q], F32, four_rows_a_partition(gout))
+        th_col = load("th_col", [P, 1], F32, th)
+        vals_s = load_scales("vals_s", vals_scales, nc.vector)
+        key_rows0 = load("key_rows0", [P, T], F32, keyrows[0:P, :])
+        reserve_col = load("reserve_col", [P, 1], F32, reserve)
+        fs_col = load("fs_col", [P, PACK], F32, four_slots_a_partition(fs))
+        key_rows1, key_rows2, key_rows3 = [
+            load("key_rows%d" % b, [P, T], F32, keyrows[b * P : (b + 1) * P, :]) for b in range(1, D // P)
+        ]
+        res_sb = load("res_sb", [P, D], F32, res)
 
-        def quantize(name, grouped, width):
-            codes = sbuf(name + "_codes", [P, width], U32)
-            scales = sbuf(name + "_scales", [P, width], U8)
-            nc.vector.quantize_mx(out=codes[:].bitcast(FP8X4), scales=scales[:], in_=grouped)
-            return codes, scales
-
-        def gather_packed(name, pool_words, pool_scales):
-            words = sbuf(name + "_words", [P, I], U16)
-            nc.vector.tensor_copy(out=words[:], in_=pool_words[:].indirect(offsets[:]))
-            scale_bytes = sbuf(name + "_bytes", [P, I], U8)
-            nc.vector.tensor_copy(out=scale_bytes[:], in_=pool_scales[:].indirect(offsets[:]))
-            return words, scale_bytes
-
-        def score(name, codes, scales, words, scale_bytes):
-            acc = ps.tile([P, I], F32, name=name + "_acc", tag=name + "_bank")
-            nc.tensor.matmul_mx(out=acc[:], lhsT=codes.bitcast(FP8X4), lhsT_scale=scales,
-                                rhs=words[:].bitcast(FP4X4), rhs_scale=scale_bytes[:], start=True, stop=True)
-            return acc
+        def quantize(codes, scales, grouped):
+            nc.vector.quantize_mx(out=codes.bitcast(FP8X4), scales=scales, in_=grouped.rearrange("p w t -> p (w t)"))
 
         def spread(name, col, bank):
             rows = ps.tile([P, PACK, P], F32, name=name, tag=bank)
-            for c in range(PACK):
-                nc.tensor.transpose(rows[:, c, :], col[:, c : c + 1].to_broadcast([P, P]), ident[:])
-            return rows[:].rearrange("p c s -> p s c")
+            for t in range(PACK):
+                nc.tensor.transpose(rows[:, t, :], col[:, t : t + 1].to_broadcast([P, P]), ident[:])
+            return rows[:].rearrange("p t s -> p s t")
 
         def by_four(tile):
-            return tile[:].rearrange("p (s c) -> p s c", c=PACK)
+            return tile[:].rearrange("p (s t) -> p s t", t=PACK)
+
+        def score(name, raw, table, pool_words, pool_scales, bank):
+            words = sbuf(table + "_words_picked", [P, I], U16)
+            nc.vector.tensor_copy(out=words[:], in_=pool_words[:].indirect(offsets[:]))
+            scale_bytes = sbuf(table + "_scales_picked", [P, I], U8)
+            nc.vector.tensor_copy(out=scale_bytes[:], in_=pool_scales[:].indirect(offsets[:]))
+            grouped = sbuf(name + "_grouped", [P, Q, PACK], BF16)
+            nc.scalar.copy(out=grouped[:], in_=raw[:].rearrange("p t w -> p w t"))
+            codes = sbuf(name + "_codes", [P, Q], U32)
+            scales = sbuf(name + "_scales", [P, Q], U8)
+            quantize(codes[:], scales[:], grouped[:])
+            acc = ps.tile([P, I], F32, name=name + "_acc", tag=bank)
+            nc.tensor.matmul_mx(out=acc[:], lhsT=codes[:].bitcast(FP8X4), lhsT_scale=scales[:],
+                                rhs=words[:].bitcast(FP4X4), rhs_scale=scale_bytes[:], start=True, stop=True)
+            return acc
+
+        def turn(name, rows, bank, grouped):
+            pairs = rows[:].bitcast(F32)
+            turned = ps.tile([P, 2, P], F32, name=name + "_turned", tag=bank)
+            for u in range(2):
+                nc.tensor.transpose(turned[:, u, :], pairs[:, u : I // 2 : 2], ident[:])
+            nc.scalar.copy(out=grouped.bitcast(F32), in_=turned[:].rearrange("p u r -> p r u"))
+
+        def gather_keys(name, rows):
+            picked = sbuf(name, [P, I], BF16)
+            nc.vector.tensor_copy(out=picked[:], in_=rows[:].indirect(offsets[:]))
+            return picked
+
+        def weighted_sum(name, total, values, weights):
+            product = sbuf(name, [P, I], F32)
+            nc.vector.scalar_tensor_tensor(out=product[:], in0=values[:], scalar=1.0, in1=weights[:],
+                                           op0=ALU.mult, op1=ALU.mult, accum_out=total[:])
 
         neg_th = sbuf("neg_th", [P, 1], F32)
         nc.scalar.activation(out=neg_th[:], in_=th_col[:], func=ACT.Copy, scale=-1.0)
+        size_rows = sbuf("size_rows", [P, I], F32)
+        nc.scalar.copy(out=by_four(size_rows), in_=spread("size_spread", size_col, "score_bank"))
 
-        a_words, a_bytes = gather_packed("a", keys_w, keys_s)
-        qg_grouped = sbuf("qg_grouped", [P, 2 * Q, PACK], BF16)
-        nc.scalar.copy(out=qg_grouped[:, 0:Q, :], in_=q_raw[:].rearrange("p j w -> p w j"))
-        nc.scalar.copy(out=qg_grouped[:, Q : 2 * Q, :], in_=g_raw[:].rearrange("p j w -> p w j"))
-        qg_codes, qg_scales = quantize("qg", qg_grouped[:].rearrange("p w j -> p (w j)"), 2 * Q)
-        a = score("a", qg_codes[:, 0:Q], qg_scales[:, 0:Q], a_words, a_bytes)
+        a = score("query", query_raw, "keys", keys_w, keys_s, "score_bank")
         sig = sbuf("sig", [P, I], F32)
         nc.scalar.activation(out=sig[:], in_=a[:], func=ACT.Sigmoid, bias=neg_th[:])
         hinge = sbuf("hinge", [P, I], F32)
@@ -140,94 +156,79 @@ def tile_attend_bsoftthreshold_q_kernel(tc, query, keys_words, keys_scales, th, 
         off_half = sbuf("off_half", [P, I], F32)
         nc.scalar.activation(out=off_half[:], in_=sig[:], func=ACT.Abs, bias=-0.5)
 
-        c_words, c_bytes = gather_packed("c", vals_w, vals_s)
-        c0 = score("c", qg_codes[:, Q : 2 * Q], qg_scales[:, Q : 2 * Q], c_words, c_bytes)
-        size_ps = spread("size_ps", small["size"], "size_ps_bank")
-        size_rows = sbuf("size_rows", [P, I], F32)
-        nc.scalar.copy(out=by_four(size_rows), in_=size_ps)
+        c0 = score("gout", gout_raw, "vals", vals_w, vals_s, "grad_bank")
 
         z_part = sbuf("z_part", [P, 1], F32)
-        nc.scalar.activation(out=z_part[:], in_=hinge_sum[:], func=ACT.Identity, bias=small["reserve"][:])
+        nc.scalar.activation(out=z_part[:], in_=hinge_sum[:], func=ACT.Identity, bias=reserve_col[:])
         log_term = sbuf("log_term", [P, I], F32)
         log_sum = sbuf("log_sum", [P, 1], F32)
         nc.scalar.activation(out=log_term[:], in_=off_half[:], func=ACT.Ln, bias=0.5, accum_out=log_sum[:])
         z = sbuf("z", [P, 1], F32)
         nc.scalar.activation(out=z[:], in_=log_sum[:], func=ACT.Identity, scale=-1.0, bias=z_part[:])
 
-        first_picked = sbuf("picked0", [P, I], BF16)
-        nc.vector.tensor_copy(out=first_picked[:], in_=key_pool[0][:].indirect(offsets[:]))
+        picked0 = gather_keys("picked0", key_rows0)
         cs = sbuf("cs", [P, I], F32)
         nc.vector.tensor_tensor(out=cs[:], in0=c0[:], in1=size_rows[:], op=ALU.mult)
-        fs_ps = spread("fs_ps", small["fs"], "c_bank")
-        scrap = sbuf("scrap", [P, I], F32)
-        s_hinge = sbuf("s_hinge", [P, 1], F32)
-        nc.vector.scalar_tensor_tensor(out=scrap[:], in0=hinge[:], scalar=1.0, in1=cs[:], op0=ALU.mult, op1=ALU.mult,
-                                       accum_out=s_hinge[:])
-        rz = sbuf("rz", [P, 1], F32)
-        nc.vector.reciprocal(out=rz[:], in_=z[:])
-        scrap2 = sbuf("scrap2", [P, I], F32)
-        s_log = sbuf("s_log", [P, 1], F32)
-        nc.vector.scalar_tensor_tensor(out=scrap2[:], in0=log_term[:], scalar=1.0, in1=cs[:], op0=ALU.mult, op1=ALU.mult,
-                                       accum_out=s_log[:])
-        wz = sbuf("wz", [P, I], F32)
-        nc.vector.scalar_tensor_tensor(out=by_four(wz), in0=by_four(sig), scalar=rz[:], in1=fs_ps, op0=ALU.mult, op1=ALU.mult)
+        fs_spread = spread("fs_spread", fs_col, "grad_bank")
+        hinge_dot = sbuf("hinge_dot", [P, 1], F32)
+        weighted_sum("hinge_product", hinge_dot, hinge, cs)
+        inv_z = sbuf("inv_z", [P, 1], F32)
+        nc.vector.reciprocal(out=inv_z[:], in_=z[:])
+        log_dot = sbuf("log_dot", [P, 1], F32)
+        weighted_sum("log_product", log_dot, log_term, cs)
+        factor = sbuf("factor", [P, I], F32)
+        nc.vector.scalar_tensor_tensor(out=by_four(factor), in0=by_four(sig), scalar=inv_z[:], in1=fs_spread,
+                                       op0=ALU.mult, op1=ALU.mult)
         mean = sbuf("mean", [P, 1], F32)
-        nc.vector.tensor_scalar(out=mean[:], in0=s_hinge[:], scalar1=s_log[:], scalar2=rz[:], op0=ALU.subtract, op1=ALU.mult)
+        nc.vector.tensor_scalar(out=mean[:], in0=hinge_dot[:], scalar1=log_dot[:], scalar2=inv_z[:],
+                                op0=ALU.subtract, op1=ALU.mult)
         gs = sbuf("gs", [P, I], BF16)
-        nc.vector.scalar_tensor_tensor(out=gs[:], in0=cs[:], scalar=mean[:], in1=wz[:], op0=ALU.subtract, op1=ALU.mult)
-
-        def turn(name, rows, bank, grouped):
-            words = rows[:].bitcast(F32)
-            turned = ps.tile([P, 2, P], F32, name=name + "_turned", tag=bank)
-            for u in range(2):
-                nc.tensor.transpose(turned[:, u, :], words[:, u : I // 2 : 2], ident[:])
-            nc.scalar.copy(out=grouped.bitcast(F32), in_=turned[:].rearrange("p u r -> p r u"))
-
-        def flat(grouped):
-            return grouped[:].rearrange("p r j -> p (r j)")
+        nc.vector.scalar_tensor_tensor(out=gs[:], in0=cs[:], scalar=mean[:], in1=factor[:],
+                                       op0=ALU.subtract, op1=ALU.mult)
 
         kt0_grouped = sbuf("kt0_grouped", [P, P, PACK], BF16)
-        turn("kt0", first_picked, "kt_bank0", kt0_grouped[:])
-        kt0_codes, kt0_scales = quantize("kt0", flat(kt0_grouped), P)
+        turn("kt0", picked0, "turn_bank0", kt0_grouped[:])
+        kt0_codes = sbuf("kt0_codes", [P, P], U32)
+        kt0_scales = sbuf("kt0_scales", [P, P], U8)
+        quantize(kt0_codes[:], kt0_scales[:], kt0_grouped[:])
 
         kt12_grouped = sbuf("kt12_grouped", [P, 2 * P, PACK], BF16)
-        cast = sbuf("cast", [P, T], BF16)
-        for piece in range(4):
-            part = slice(piece * 512, (piece + 1) * 512)
-            nc.scalar.activation(out=cast[:, part], in_=key_pool[1][:, part], func=ACT.Copy)
+        cast_rows = sbuf("cast_rows", [P, T], BF16)
+        for first in range(0, T, CAST_PIECE):
+            piece = slice(first, first + CAST_PIECE)
+            nc.scalar.activation(out=cast_rows[:, piece], in_=key_rows1[:, piece], func=ACT.Copy)
         picked1 = sbuf("picked1", [P, I], BF16)
-        nc.scalar.activation(out=picked1[:], in_=cast[:].indirect(offsets[:]), func=ACT.Copy)
+        nc.scalar.activation(out=picked1[:], in_=cast_rows[:].indirect(offsets[:]), func=ACT.Copy)
 
-        picked2 = sbuf("picked2", [P, I], BF16)
-        nc.vector.tensor_copy(out=picked2[:], in_=key_pool[2][:].indirect(offsets[:]))
-
+        picked2 = gather_keys("picked2", key_rows2)
         gs_grouped = sbuf("gs_grouped", [P, Q, PACK], BF16)
-        turn("gs", gs, "size_ps_bank", gs_grouped[:])
-
-        picked3 = sbuf("picked3", [P, I], BF16)
-        nc.vector.tensor_copy(out=picked3[:], in_=key_pool[3][:].indirect(offsets[:]))
-
-        turn("kt1", picked1, "kt_bank1", kt12_grouped[:, 0:P, :])
-        turn("kt2", picked2, "kt_bank0", kt12_grouped[:, P : 2 * P, :])
+        turn("gs", gs, "score_bank", gs_grouped[:])
+        picked3 = gather_keys("picked3", key_rows3)
+        turn("kt2", picked2, "turn_bank0", kt12_grouped[:, P : 2 * P, :])
+        turn("kt1", picked1, "turn_bank1", kt12_grouped[:, 0:P, :])
         kt3_grouped = sbuf("kt3_grouped", [P, P, PACK], BF16)
-        turn("kt3", picked3, "kt_bank1", kt3_grouped[:])
+        turn("kt3", picked3, "turn_bank2", kt3_grouped[:])
 
         late_codes = sbuf("late_codes", [P, 4 * P], U32)
         late_scales = sbuf("late_scales", [P, 4 * P], U8)
-        gs_codes, gs_scales = late_codes[:, 3 * P :], late_scales[:, 3 * P :]
-        nc.vector.quantize_mx(out=gs_codes.bitcast(FP8X4), scales=gs_scales, in_=flat(gs_grouped))
-        nc.vector.quantize_mx(out=late_codes[:, 0 : 2 * P].bitcast(FP8X4), scales=late_scales[:, 0 : 2 * P], in_=flat(kt12_grouped))
-        nc.vector.quantize_mx(out=late_codes[:, 2 * P : 3 * P].bitcast(FP8X4), scales=late_scales[:, 2 * P : 3 * P], in_=flat(kt3_grouped))
+        kt12_cols, kt3_cols, gs_cols = slice(0, 2 * P), slice(2 * P, 3 * P), slice(3 * P, 4 * P)
+        quantize(late_codes[:, gs_cols], late_scales[:, gs_cols], gs_grouped[:])
+        quantize(late_codes[:, kt12_cols], late_scales[:, kt12_cols], kt12_grouped[:])
+        quantize(late_codes[:, kt3_cols], late_scales[:, kt3_cols], kt3_grouped[:])
 
-        for name, cols, codes, scales, bank in (
-            ("o0", slice(0, P), kt0_codes[:], kt0_scales[:], "a_bank"),
-            ("o1", slice(P, 3 * P), late_codes[:, 0 : 2 * P], late_scales[:, 0 : 2 * P], "c_bank"),
-            ("o2", slice(3 * P, D), late_codes[:, 2 * P : 3 * P], late_scales[:, 2 * P : 3 * P], "last_bank"),
-        ):
-            width = cols.stop - cols.start
-            acc = ps.tile([P, width], F32, name=name + "_acc", tag=bank)
-            nc.tensor.matmul_mx(out=acc[:], lhsT=gs_codes.bitcast(FP8X4), lhsT_scale=gs_scales,
+        def product_with_gs(acc, codes, scales):
+            nc.tensor.matmul_mx(out=acc, lhsT=late_codes[:, gs_cols].bitcast(FP8X4), lhsT_scale=late_scales[:, gs_cols],
                                 rhs=codes.bitcast(FP8X4), rhs_scale=scales, start=True, stop=True)
-            result = sbuf(name, [P, width], F32)
+
+        def add_residual_and_store(name, acc, cols):
+            result = sbuf(name, [P, cols.stop - cols.start], F32)
             nc.vector.tensor_tensor(out=result[:], in0=acc[:], in1=res_sb[:, cols], op=ALU.add)
             nc.sync.dma_start(out=out[:, cols], in_=result[:])
+
+        early_acc = ps.tile([P, 3 * P], F32, name="early_acc", tag="early_bank")
+        product_with_gs(early_acc[:, 0:P], kt0_codes[:], kt0_scales[:])
+        product_with_gs(early_acc[:, P : 3 * P], late_codes[:, kt12_cols], late_scales[:, kt12_cols])
+        last_acc = ps.tile([P, P], F32, name="last_acc", tag="last_bank")
+        product_with_gs(last_acc[:], late_codes[:, kt3_cols], late_scales[:, kt3_cols])
+        add_residual_and_store("out_early", early_acc, slice(0, 3 * P))
+        add_residual_and_store("out_last", last_acc, slice(3 * P, D))

from contextlib import ExitStack

import concourse.mybir as mybir
from concourse.masks import make_identity

D, T, I, Q = 512, 2048, 512, 128
FLOPS = 3 * 2 * Q * D * I

F32 = mybir.dt.float32
BF16 = mybir.dt.bfloat16
I32 = mybir.dt.int32
U32 = mybir.dt.uint32
U16 = mybir.dt.uint16
U8 = mybir.dt.uint8
FP8X4 = mybir.dt.float8_e4m3fn_x4
FP4X4 = mybir.dt.float4_e2m1fn_x4
ACT = mybir.ActivationFunctionType
ALU = mybir.AluOpType

P = 128
PACK = 4
QUADRANTS = 4
CAST_PIECE = 512

TAKES_OVER = {
    "vals_words_picked": "query_raw",
    "gout_grouped": "size_col",
    "log_term": "gout_raw",
    "cs": "key_rows0",
    "cast_rows": "off_half",
    "log_product": "log_sum",
    "kt0_grouped": "z_part",
    "kt0_codes": "log_sum",
    "picked2": "log_dot",
    "gs_grouped": "key_rows1",
    "late_codes": "key_rows3",
    "out_early": "kt3_grouped",
}


def tile_attend_bsoftthreshold_q_kernel(tc, query, keys_words, keys_scales, th, reserve, gout,
                                         vals_words, vals_scales, size, fs, keyrows, res, offs, out):
    nc = tc.nc
    with ExitStack() as ctx:
        sb = ctx.enter_context(tc.tile_pool(name="sb", bufs=1))
        ps = ctx.enter_context(tc.psum_pool(name="ps", bufs=1))

        def sbuf(name, shape, dtype):
            return sb.tile(shape, dtype, name=name, tag=TAKES_OVER.get(name, name), align_bytes=64)

        def load(name, shape, dtype, src):
            tile = sbuf(name, shape, dtype)
            nc.sync.dma_start(out=tile[:], in_=src)
            return tile

        def load_words(name, words):
            tile = sbuf(name, [P, T], U16)
            nc.sync.dma_start(out=tile[:].bitcast(I32), in_=words[0].bitcast(I32))
            return tile

        def load_scales(name, scales, second_half_engine):
            tile = sbuf(name, [P, T], U8)
            nc.vector.memset(tile[:, : T // 2].bitcast(I32), 0)
            second_half_engine.memset(tile[:, T // 2 :].bitcast(I32), 0)
            for quad in range(QUADRANTS):
                nc.sync.dma_start(out=tile[32 * quad : 32 * quad + 4, :].bitcast(I32),
                                  in_=scales[0, 4 * quad : 4 * quad + 4, :].bitcast(I32))
            return tile

        def four_rows_a_partition(rows):
            return rows.rearrange("(p t) w -> p t w", t=PACK)

        def four_slots_a_partition(row):
            return row.rearrange("o (p t) -> p (o t)", t=PACK)

        offsets = load("offsets", [P, I // 16], U16, offs)
        keys_w = load_words("keys_w", keys_words)
        keys_s = load_scales("keys_s", keys_scales, nc.gpsimd)

        warm_in = sbuf("warm_in", [P, 1], F32)
        nc.gpsimd.memset(warm_in[:], 0.0)
        warm_out = sbuf("warm_out", [P, 1], F32)
        nc.scalar.activation(out=warm_out[:], in_=warm_in[:], func=ACT.Sigmoid)
        ident = sbuf("ident", [P, P], F32)
        make_identity(nc, ident[:])

        query_raw = load("query_raw", [P, PACK, Q], F32, four_rows_a_partition(query))
        size_col = load("size_col", [P, PACK], F32, four_slots_a_partition(size))
        vals_w = load_words("vals_w", vals_words)
        gout_raw = load("gout_raw", [P, PACK, Q], F32, four_rows_a_partition(gout))
        th_col = load("th_col", [P, 1], F32, th)
        vals_s = load_scales("vals_s", vals_scales, nc.vector)
        key_rows0 = load("key_rows0", [P, T], F32, keyrows[0:P, :])
        reserve_col = load("reserve_col", [P, 1], F32, reserve)
        fs_col = load("fs_col", [P, PACK], F32, four_slots_a_partition(fs))
        key_rows1, key_rows2, key_rows3 = [
            load("key_rows%d" % b, [P, T], F32, keyrows[b * P : (b + 1) * P, :]) for b in range(1, D // P)
        ]
        res_sb = load("res_sb", [P, D], F32, res)

        def quantize(codes, scales, grouped):
            nc.vector.quantize_mx(out=codes.bitcast(FP8X4), scales=scales, in_=grouped.rearrange("p w t -> p (w t)"))

        def spread(name, col, bank):
            rows = ps.tile([P, PACK, P], F32, name=name, tag=bank)
            for t in range(PACK):
                nc.tensor.transpose(rows[:, t, :], col[:, t : t + 1].to_broadcast([P, P]), ident[:])
            return rows[:].rearrange("p t s -> p s t")

        def by_four(tile):
            return tile[:].rearrange("p (s t) -> p s t", t=PACK)

        def score(name, raw, table, pool_words, pool_scales, bank):
            words = sbuf(table + "_words_picked", [P, I], U16)
            nc.vector.tensor_copy(out=words[:], in_=pool_words[:].indirect(offsets[:]))
            scale_bytes = sbuf(table + "_scales_picked", [P, I], U8)
            nc.vector.tensor_copy(out=scale_bytes[:], in_=pool_scales[:].indirect(offsets[:]))
            grouped = sbuf(name + "_grouped", [P, Q, PACK], BF16)
            nc.scalar.copy(out=grouped[:], in_=raw[:].rearrange("p t w -> p w t"))
            codes = sbuf(name + "_codes", [P, Q], U32)
            scales = sbuf(name + "_scales", [P, Q], U8)
            quantize(codes[:], scales[:], grouped[:])
            acc = ps.tile([P, I], F32, name=name + "_acc", tag=bank)
            nc.tensor.matmul_mx(out=acc[:], lhsT=codes[:].bitcast(FP8X4), lhsT_scale=scales[:],
                                rhs=words[:].bitcast(FP4X4), rhs_scale=scale_bytes[:], start=True, stop=True)
            return acc

        def turn(name, rows, bank, grouped):
            pairs = rows[:].bitcast(F32)
            turned = ps.tile([P, 2, P], F32, name=name + "_turned", tag=bank)
            for u in range(2):
                nc.tensor.transpose(turned[:, u, :], pairs[:, u : I // 2 : 2], ident[:])
            nc.scalar.copy(out=grouped.bitcast(F32), in_=turned[:].rearrange("p u r -> p r u"))

        def gather_keys(name, rows):
            picked = sbuf(name, [P, I], BF16)
            nc.vector.tensor_copy(out=picked[:], in_=rows[:].indirect(offsets[:]))
            return picked

        def weighted_sum(name, total, values, weights):
            product = sbuf(name, [P, I], F32)
            nc.vector.scalar_tensor_tensor(out=product[:], in0=values[:], scalar=1.0, in1=weights[:],
                                           op0=ALU.mult, op1=ALU.mult, accum_out=total[:])

        neg_th = sbuf("neg_th", [P, 1], F32)
        nc.scalar.activation(out=neg_th[:], in_=th_col[:], func=ACT.Copy, scale=-1.0)
        size_rows = sbuf("size_rows", [P, I], F32)
        nc.scalar.copy(out=by_four(size_rows), in_=spread("size_spread", size_col, "score_bank"))

        a = score("query", query_raw, "keys", keys_w, keys_s, "score_bank")
        sig = sbuf("sig", [P, I], F32)
        nc.scalar.activation(out=sig[:], in_=a[:], func=ACT.Sigmoid, bias=neg_th[:])
        hinge = sbuf("hinge", [P, I], F32)
        hinge_sum = sbuf("hinge_sum", [P, 1], F32)
        nc.scalar.activation(out=hinge[:], in_=a[:], func=ACT.Relu, bias=neg_th[:], accum_out=hinge_sum[:])
        off_half = sbuf("off_half", [P, I], F32)
        nc.scalar.activation(out=off_half[:], in_=sig[:], func=ACT.Abs, bias=-0.5)

        c0 = score("gout", gout_raw, "vals", vals_w, vals_s, "grad_bank")

        z_part = sbuf("z_part", [P, 1], F32)
        nc.scalar.activation(out=z_part[:], in_=hinge_sum[:], func=ACT.Identity, bias=reserve_col[:])
        log_term = sbuf("log_term", [P, I], F32)
        log_sum = sbuf("log_sum", [P, 1], F32)
        nc.scalar.activation(out=log_term[:], in_=off_half[:], func=ACT.Ln, bias=0.5, accum_out=log_sum[:])
        z = sbuf("z", [P, 1], F32)
        nc.scalar.activation(out=z[:], in_=log_sum[:], func=ACT.Identity, scale=-1.0, bias=z_part[:])

        picked0 = gather_keys("picked0", key_rows0)
        cs = sbuf("cs", [P, I], F32)
        nc.vector.tensor_tensor(out=cs[:], in0=c0[:], in1=size_rows[:], op=ALU.mult)
        fs_spread = spread("fs_spread", fs_col, "grad_bank")
        hinge_dot = sbuf("hinge_dot", [P, 1], F32)
        weighted_sum("hinge_product", hinge_dot, hinge, cs)
        inv_z = sbuf("inv_z", [P, 1], F32)
        nc.vector.reciprocal(out=inv_z[:], in_=z[:])
        log_dot = sbuf("log_dot", [P, 1], F32)
        weighted_sum("log_product", log_dot, log_term, cs)
        factor = sbuf("factor", [P, I], F32)
        nc.vector.scalar_tensor_tensor(out=by_four(factor), in0=by_four(sig), scalar=inv_z[:], in1=fs_spread,
                                       op0=ALU.mult, op1=ALU.mult)
        mean = sbuf("mean", [P, 1], F32)
        nc.vector.tensor_scalar(out=mean[:], in0=hinge_dot[:], scalar1=log_dot[:], scalar2=inv_z[:],
                                op0=ALU.subtract, op1=ALU.mult)
        gs = sbuf("gs", [P, I], BF16)
        nc.vector.scalar_tensor_tensor(out=gs[:], in0=cs[:], scalar=mean[:], in1=factor[:],
                                       op0=ALU.subtract, op1=ALU.mult)

        kt0_grouped = sbuf("kt0_grouped", [P, P, PACK], BF16)
        turn("kt0", picked0, "turn_bank0", kt0_grouped[:])
        kt0_codes = sbuf("kt0_codes", [P, P], U32)
        kt0_scales = sbuf("kt0_scales", [P, P], U8)
        quantize(kt0_codes[:], kt0_scales[:], kt0_grouped[:])

        kt12_grouped = sbuf("kt12_grouped", [P, 2 * P, PACK], BF16)
        cast_rows = sbuf("cast_rows", [P, T], BF16)
        for first in range(0, T, CAST_PIECE):
            piece = slice(first, first + CAST_PIECE)
            nc.scalar.activation(out=cast_rows[:, piece], in_=key_rows1[:, piece], func=ACT.Copy)
        picked1 = sbuf("picked1", [P, I], BF16)
        nc.scalar.activation(out=picked1[:], in_=cast_rows[:].indirect(offsets[:]), func=ACT.Copy)

        picked2 = gather_keys("picked2", key_rows2)
        gs_grouped = sbuf("gs_grouped", [P, Q, PACK], BF16)
        turn("gs", gs, "score_bank", gs_grouped[:])
        picked3 = gather_keys("picked3", key_rows3)
        turn("kt2", picked2, "turn_bank0", kt12_grouped[:, P : 2 * P, :])
        turn("kt1", picked1, "turn_bank1", kt12_grouped[:, 0:P, :])
        kt3_grouped = sbuf("kt3_grouped", [P, P, PACK], BF16)
        turn("kt3", picked3, "turn_bank2", kt3_grouped[:])

        late_codes = sbuf("late_codes", [P, 4 * P], U32)
        late_scales = sbuf("late_scales", [P, 4 * P], U8)
        kt12_cols, kt3_cols, gs_cols = slice(0, 2 * P), slice(2 * P, 3 * P), slice(3 * P, 4 * P)
        quantize(late_codes[:, gs_cols], late_scales[:, gs_cols], gs_grouped[:])
        quantize(late_codes[:, kt12_cols], late_scales[:, kt12_cols], kt12_grouped[:])
        quantize(late_codes[:, kt3_cols], late_scales[:, kt3_cols], kt3_grouped[:])

        def product_with_gs(acc, codes, scales):
            nc.tensor.matmul_mx(out=acc, lhsT=late_codes[:, gs_cols].bitcast(FP8X4), lhsT_scale=late_scales[:, gs_cols],
                                rhs=codes.bitcast(FP8X4), rhs_scale=scales, start=True, stop=True)

        def add_residual_and_store(name, acc, cols):
            result = sbuf(name, [P, cols.stop - cols.start], F32)
            nc.vector.tensor_tensor(out=result[:], in0=acc[:], in1=res_sb[:, cols], op=ALU.add)
            nc.sync.dma_start(out=out[:, cols], in_=result[:])

        early_acc = ps.tile([P, 3 * P], F32, name="early_acc", tag="early_bank")
        product_with_gs(early_acc[:, 0:P], kt0_codes[:], kt0_scales[:])
        product_with_gs(early_acc[:, P : 3 * P], late_codes[:, kt12_cols], late_scales[:, kt12_cols])
        last_acc = ps.tile([P, P], F32, name="last_acc", tag="last_bank")
        product_with_gs(last_acc[:], late_codes[:, kt3_cols], late_scales[:, kt3_cols])
        add_residual_and_store("out_early", early_acc, slice(0, 3 * P))
        add_residual_and_store("out_last", last_acc, slice(3 * P, D))
